import numpy as np
import ml_dtypes


def mxq(x, axis, fmt="e4m3"):
    dtype, down = {"e4m3": (ml_dtypes.float8_e4m3fn, 7), "e5m2": (ml_dtypes.float8_e5m2, 14)}[fmt]
    v = np.moveaxis(np.asarray(x, np.float32).astype(ml_dtypes.bfloat16).astype(np.float64), axis, -1)
    blocks = v.reshape(v.shape[:-1] + (-1, 32))
    amax = np.abs(blocks).max(-1, keepdims=True)
    byte = np.maximum(np.where(amax > 0, np.frexp(amax)[1] - 1 + 127, 0) - down, 1)
    scale = np.exp2(byte - 127.0)
    codes = (blocks / scale).astype(np.float32).astype(dtype).astype(np.float64)
    return np.moveaxis((codes * scale).reshape(v.shape), -1, axis)


WIDE = False


def mx_kscale(k):
    if not WIDE:
        return np.ones(k)
    levels = np.array([10, -10, 5, -5, 0])
    if k % 512:
        return np.exp2(np.random.permutation(np.resize(levels, k // 32))).repeat(32)
    a = np.empty((k // 512, 16))
    for p in range(k // 512):
        a[p, :8] = np.random.permutation(np.resize(levels, 8))
        for g in range(8):
            far = levels[np.abs(levels - a[p, g]) >= 10]
            a[p, g + 8] = far[np.random.randint(len(far))]
    return np.exp2(a.ravel()).repeat(32)


def f64(x):
    return np.asarray(x).astype(np.float64)


def striped(idx):
    return np.tile(idx.reshape(-1, 16).T, (8, 1)).astype(np.uint16)


def unstriped(offs):
    return offs[:16].T.reshape(-1).astype(np.int64)


def pack_weight(w):
    k, n = w.shape
    w = f64(np.asarray(w, np.float32).astype(ml_dtypes.bfloat16)).reshape(k // 32, 32, n)
    amax = np.abs(w).max(1)
    byte = np.clip(np.where(amax > 0, np.frexp(amax)[1] - 1 + 127 - 7, 1), 1, 254)
    scaled = (w * np.exp2(127.0 - byte)[:, None, :]).reshape(k, n).astype(np.float32)
    words = np.ascontiguousarray(scaled.reshape(k // 512, 128, 4, n).transpose(0, 1, 3, 2)).astype(ml_dtypes.float8_e4m3fn).view(np.uint8)
    return words, np.ascontiguousarray(byte.astype(np.uint8).reshape(k // 512, 16, n))


def unpack_weight(words, scales):
    g, p, n, _ = words.shape
    vals = np.ascontiguousarray(words).view(ml_dtypes.float8_e4m3fn).astype(np.float64) * np.repeat(np.exp2(scales.astype(np.float64) - 127.0), 8, axis=1)[..., None]
    return vals.transpose(0, 1, 3, 2).reshape(g * 512, n)


K, T, S, D, N, V = 512, 2048, 512, 8, 128, 64
P = 2 ** 7


def setup_inputs():
    n = np.random.standard_normal
    s = mx_kscale(K)[:, None]
    packed_xT = pack_weight(n((K, T)) * s)
    return {
        "x_words": packed_xT[0],
        "x_scales": packed_xT[1],
        "w1": (n((K, N)) / np.sqrt(K) / s).astype(np.float32),
        "occ": (np.tile(np.random.uniform(0.1, 2.0, S) / D, (P, 1))).astype(np.float32),
        "corr": (np.tile(np.random.uniform(0.35, 0.55, V), (P, 1))).astype(np.float32),
        "offs": striped(np.random.permutation(T)[:S]),
    }


def reference(x_words, x_scales, w1, occ, corr, offs):
    xq = unpack_weight(x_words, x_scales)[:, unstriped(offs)]
    y = mxq(f64(w1), 0, "e4m3").T @ xq
    oc = ((y) ** 2) * f64(occ)[:1]
    dens = oc.reshape(len(oc), -1, D).sum(axis=2) + 0.02
    lr = np.log(dens)
    rs = 0.62 * np.exp(-0.3333 * lr)
    return -0.738 * np.exp(1.3333 * lr) - (dens * (f64(corr)[:1] / (rs + 0.8)))

@@ -1,0 +1,120 @@
+from contextlib import ExitStack
+
+import concourse.mybir as mybir
+
+K, T, S, D, M, V = 512, 2048, 512, 8, 128, 64
+FLOPS = 2 * K * M * S
+
+F32 = mybir.dt.float32
+BF16 = mybir.dt.bfloat16
+I32 = mybir.dt.int32
+U32 = mybir.dt.uint32
+U16 = mybir.dt.uint16
+U8 = mybir.dt.uint8
+FP8X4 = mybir.dt.float8_e4m3fn_x4
+ALU = mybir.AluOpType
+ACT = mybir.ActivationFunctionType
+AXIS = mybir.AxisListType
+
+P = 128
+PACK = 4
+PIECE = 128
+LIST_ROWS = 16
+
+
+def tile_picked_ylda_en_p_kernel(
+    tc, x_words, x_scales, w1, occ, corr, offs, out
+):
+    nc = tc.nc
+    with ExitStack() as ctx:
+        keep = ctx.enter_context(tc.tile_pool(name="keep", bufs=1))
+        psum = ctx.enter_context(tc.psum_pool(name="psum", bufs=1))
+
+        scale_table = keep.tile([P, T], U8, align_bytes=64)
+        nc.vector.memset(scale_table[:].bitcast(I32), 0)
+
+        w_raw = keep.tile([P, PACK, M], F32)
+        nc.sync.dma_start(out=w_raw[:], in_=w1.rearrange("(p j) m -> p j m", j=PACK))
+        offsets = keep.tile([P, S // LIST_ROWS], U16)
+        nc.sync.dma_start(offsets[:], offs)
+        for j in range(4):
+            nc.sync.dma_start(
+                out=scale_table[j:P:32, :].bitcast(I32),
+                in_=x_scales[0, j:16:4, :].bitcast(I32),
+            )
+        word_table = keep.tile([P, T], I32, align_bytes=64)
+        nc.sync.dma_start(
+            out=word_table[:], in_=x_words[0].rearrange("p n t -> p (n t)").bitcast(I32)
+        )
+        occ_sb = keep.tile([P, S], F32)
+        nc.sync.dma_start(out=occ_sb[:], in_=occ)
+        corr_sb = keep.tile([P, V], F32)
+        nc.sync.dma_start(out=corr_sb[:], in_=corr)
+
+        ones = keep.tile([P, 1], F32)
+        nc.gpsimd.memset(ones[:], 1.0)
+        tanh_bias = keep.tile([P, 1], F32)
+        nc.scalar.activation(out=tanh_bias[:], in_=ones[:], func=ACT.Ln, scale=(0.8 / 0.62) ** 0.5)
+
+        w_bf = keep.tile([P, M, PACK], BF16, align_bytes=64)
+        nc.vector.tensor_copy(out=w_bf[:], in_=w_raw[:].rearrange("p j m -> p m j"))
+        w_codes = keep.tile([P, M], U32, align_bytes=64)
+        w_scales = keep.tile([P, M], U8, align_bytes=64)
+        nc.vector.quantize_mx(
+            out=w_codes[:].bitcast(FP8X4),
+            scales=w_scales[:],
+            in_=w_bf[:].rearrange("p m j -> p (m j)"),
+        )
+
+        x_scale_plane = keep.tile([P, S], U8, align_bytes=64)
+        nc.vector.tensor_copy(x_scale_plane[:], scale_table[:].indirect(offsets[:]))
+
+        pieces = range(S // PIECE)
+        x_codes = [keep.tile([P, PIECE], U32, align_bytes=64, name=f"x_codes{i}") for i in pieces]
+        for i in pieces:
+            cols = slice(i * PIECE // LIST_ROWS, (i + 1) * PIECE // LIST_ROWS)
+            nc.vector.tensor_copy(x_codes[i][:], word_table[:].bitcast(U32).indirect(offsets[:, cols]))
+
+        sums = keep.tile([P, V], F32)
+        for i in pieces:
+            cols = slice(i * PIECE, (i + 1) * PIECE)
+            y = psum.tile([M, PIECE], F32, name=f"y{i}")
+            nc.tensor.matmul_mx(
+                out=y[:],
+                lhsT=w_codes[:].bitcast(FP8X4),
+                lhsT_scale=w_scales[:],
+                rhs=x_codes[i][:].bitcast(FP8X4),
+                rhs_scale=x_scale_plane[:, cols],
+                start=True,
+                stop=True,
+            )
+            squares = keep.tile([M, PIECE], F32, name=f"squares{i}")
+            nc.scalar.activation(out=squares[:], in_=y[:], func=ACT.Square)
+            weighted = keep.tile([M, PIECE], F32, name=f"weighted{i}")
+            nc.vector.tensor_tensor(weighted[:], squares[:], occ_sb[:, cols], ALU.mult)
+            points = slice(i * PIECE // D, (i + 1) * PIECE // D)
+            nc.vector.tensor_reduce(
+                out=sums[:, points],
+                in_=weighted[:].rearrange("p (v d) -> p v d", d=D),
+                axis=AXIS.X,
+                op=ALU.add,
+            )
+
+        log_dens = keep.tile([M, V], F32)
+        nc.scalar.activation(out=log_dens[:], in_=sums[:], func=ACT.Ln, bias=0.02)
+        dens_corr = keep.tile([M, V], F32)
+        nc.vector.scalar_tensor_tensor(dens_corr[:], sums[:], 0.02, corr_sb[:], ALU.add, ALU.mult)
+        half_limit = keep.tile([M, V], F32)
+        nc.vector.tensor_scalar(half_limit[:], dens_corr[:], -0.5 / 0.8, None, ALU.mult)
+
+        tanh_term = keep.tile([M, V], F32)
+        nc.scalar.activation(
+            out=tanh_term[:], in_=log_dens[:], func=ACT.Tanh, scale=0.3333 / 2, bias=tanh_bias[:]
+        )
+        power = keep.tile([M, V], F32)
+        nc.scalar.activation(out=power[:], in_=log_dens[:], func=ACT.Exp, scale=1.3333)
+        correlation = keep.tile([M, V], F32)
+        nc.vector.scalar_tensor_tensor(correlation[:], tanh_term[:], 1.0, half_limit[:], ALU.add, ALU.mult)
+        result = keep.tile([M, V], F32)
+        nc.vector.scalar_tensor_tensor(result[:], power[:], -0.738, correlation[:], ALU.mult, ALU.add)
+        nc.sync.dma_start(out=out, in_=result[:])

@@ -31,17 +31,14 @@ def tile_picked_ylda_en_p_kernel(
         psum = ctx.enter_context(tc.psum_pool(name="psum", bufs=1))
 
         scale_table = keep.tile([P, T], U8, align_bytes=64)
-        nc.vector.memset(scale_table[:].bitcast(I32), 0)
-
-        w_raw = keep.tile([P, PACK, M], F32)
-        nc.sync.dma_start(out=w_raw[:], in_=w1.rearrange("(p j) m -> p j m", j=PACK))
+        nc.sync.dma_start(out=scale_table[P - 16 :, :].bitcast(I32), in_=x_scales[0].bitcast(I32))
         offsets = keep.tile([P, S // LIST_ROWS], U16)
         nc.sync.dma_start(offsets[:], offs)
-        for j in range(4):
-            nc.sync.dma_start(
-                out=scale_table[j:P:32, :].bitcast(I32),
-                in_=x_scales[0, j:16:4, :].bitcast(I32),
-            )
+        nc.vector.memset(scale_table[: P - 16, :].bitcast(I32), 0)
+        x_scale_plane = keep.tile([P, S], U8, align_bytes=64)
+        nc.vector.memset(x_scale_plane[:].bitcast(I32), 0)
+        w_raw = keep.tile([P, PACK, M], F32)
+        nc.sync.dma_start(out=w_raw[:], in_=w1.rearrange("(p j) m -> p j m", j=PACK))
         word_table = keep.tile([P, T], I32, align_bytes=64)
         nc.sync.dma_start(
             out=word_table[:], in_=x_words[0].rearrange("p n t -> p (n t)").bitcast(I32)
@@ -56,6 +53,14 @@ def tile_picked_ylda_en_p_kernel(
         tanh_bias = keep.tile([P, 1], F32)
         nc.scalar.activation(out=tanh_bias[:], in_=ones[:], func=ACT.Ln, scale=(0.8 / 0.62) ** 0.5)
 
+        picked_scales = keep.tile([P, S], U8, align_bytes=64)
+        nc.vector.tensor_copy(picked_scales[:], scale_table[:].indirect(offsets[:]))
+        for j in range(4):
+            nc.scalar.dma_start(
+                out=x_scale_plane[j:P:32, :].bitcast(I32),
+                in_=picked_scales[P - 16 + j : P : 4, :].bitcast(I32),
+            )
+
         w_bf = keep.tile([P, M, PACK], BF16, align_bytes=64)
         nc.vector.tensor_copy(out=w_bf[:], in_=w_raw[:].rearrange("p j m -> p m j"))
         w_codes = keep.tile([P, M], U32, align_bytes=64)
@@ -66,8 +71,6 @@ def tile_picked_ylda_en_p_kernel(
             in_=w_bf[:].rearrange("p m j -> p (m j)"),
         )
 
-        x_scale_plane = keep.tile([P, S], U8, align_bytes=64)
-        nc.vector.tensor_copy(x_scale_plane[:], scale_table[:].indirect(offsets[:]))
 
         pieces = range(S // PIECE)
         x_codes = [keep.tile([P, PIECE], U32, align_bytes=64, name=f"x_codes{i}") for i in pieces]

@@ -38,15 +38,15 @@ def tile_picked_ylda_en_p_kernel(
         x_scale_plane = keep.tile([P, S], U8, align_bytes=64)
         nc.vector.memset(x_scale_plane[:].bitcast(I32), 0)
         w_raw = keep.tile([P, PACK, M], F32)
-        nc.sync.dma_start(out=w_raw[:], in_=w1.rearrange("(p j) m -> p j m", j=PACK))
+        nc.scalar.dma_start(out=w_raw[:], in_=w1.rearrange("(p j) m -> p j m", j=PACK))
         word_table = keep.tile([P, T], I32, align_bytes=64)
-        nc.sync.dma_start(
+        nc.scalar.dma_start(
             out=word_table[:], in_=x_words[0].rearrange("p n t -> p (n t)").bitcast(I32)
         )
         occ_sb = keep.tile([P, S], F32)
-        nc.sync.dma_start(out=occ_sb[:], in_=occ)
+        nc.scalar.dma_start(out=occ_sb[:], in_=occ)
         corr_sb = keep.tile([P, V], F32)
-        nc.sync.dma_start(out=corr_sb[:], in_=corr)
+        nc.scalar.dma_start(out=corr_sb[:], in_=corr)
 
         ones = keep.tile([P, 1], F32)
         nc.gpsimd.memset(ones[:], 1.0)
@@ -56,13 +56,13 @@ def tile_picked_ylda_en_p_kernel(
         picked_scales = keep.tile([P, S], U8, align_bytes=64)
         nc.vector.tensor_copy(picked_scales[:], scale_table[:].indirect(offsets[:]))
         for j in range(4):
-            nc.scalar.dma_start(
+            nc.sync.dma_start(
                 out=x_scale_plane[j:P:32, :].bitcast(I32),
                 in_=picked_scales[P - 16 + j : P : 4, :].bitcast(I32),
             )
 
         w_bf = keep.tile([P, M, PACK], BF16, align_bytes=64)
-        nc.vector.tensor_copy(out=w_bf[:], in_=w_raw[:].rearrange("p j m -> p m j"))
+        nc.scalar.copy(out=w_bf[:], in_=w_raw[:].rearrange("p j m -> p m j"))
         w_codes = keep.tile([P, M], U32, align_bytes=64)
         w_scales = keep.tile([P, M], U8, align_bytes=64)
         nc.vector.quantize_mx(
@@ -79,6 +79,16 @@ def tile_picked_ylda_en_p_kernel(
             nc.vector.tensor_copy(x_codes[i][:], word_table[:].bitcast(U32).indirect(offsets[:, cols]))
 
         sums = keep.tile([P, V], F32)
+        weighted_tiles = []
+
+        def add_up(i):
+            nc.vector.tensor_reduce(
+                out=sums[:, i * PIECE // D : (i + 1) * PIECE // D],
+                in_=weighted_tiles[i][:].rearrange("p (v d) -> p v d", d=D),
+                axis=AXIS.X,
+                op=ALU.add,
+            )
+
         for i in pieces:
             cols = slice(i * PIECE, (i + 1) * PIECE)
             y = psum.tile([M, PIECE], F32, name=f"y{i}")
@@ -95,13 +105,10 @@ def tile_picked_ylda_en_p_kernel(
             nc.scalar.activation(out=squares[:], in_=y[:], func=ACT.Square)
             weighted = keep.tile([M, PIECE], F32, name=f"weighted{i}")
             nc.vector.tensor_tensor(weighted[:], squares[:], occ_sb[:, cols], ALU.mult)
-            points = slice(i * PIECE // D, (i + 1) * PIECE // D)
-            nc.vector.tensor_reduce(
-                out=sums[:, points],
-                in_=weighted[:].rearrange("p (v d) -> p v d", d=D),
-                axis=AXIS.X,
-                op=ALU.add,
-            )
+            weighted_tiles.append(weighted)
+            if i > 0:
+                add_up(i - 1)
+        add_up(pieces[-1])
 
         log_dens = keep.tile([M, V], F32)
         nc.scalar.activation(out=log_dens[:], in_=sums[:], func=ACT.Ln, bias=0.02)

@@ -31,22 +31,20 @@ def tile_picked_ylda_en_p_kernel(
         psum = ctx.enter_context(tc.psum_pool(name="psum", bufs=1))
 
         scale_table = keep.tile([P, T], U8, align_bytes=64)
-        nc.sync.dma_start(out=scale_table[P - 16 :, :].bitcast(I32), in_=x_scales[0].bitcast(I32))
+        nc.scalar.dma_start(out=scale_table[P - 16 :, :].bitcast(I32), in_=x_scales[0].bitcast(I32))
         offsets = keep.tile([P, S // LIST_ROWS], U16)
         nc.sync.dma_start(offsets[:], offs)
         nc.vector.memset(scale_table[: P - 16, :].bitcast(I32), 0)
         x_scale_plane = keep.tile([P, S], U8, align_bytes=64)
         nc.vector.memset(x_scale_plane[:].bitcast(I32), 0)
-        w_raw = keep.tile([P, PACK, M], F32)
-        nc.scalar.dma_start(out=w_raw[:], in_=w1.rearrange("(p j) m -> p j m", j=PACK))
+        w_raw = keep.tile([P, PACK, M], F32, tag="staging")
+        nc.sync.dma_start(out=w_raw[:], in_=w1.rearrange("(p j) m -> p j m", j=PACK))
         word_table = keep.tile([P, T], I32, align_bytes=64)
-        nc.scalar.dma_start(
+        nc.sync.dma_start(
             out=word_table[:], in_=x_words[0].rearrange("p n t -> p (n t)").bitcast(I32)
         )
-        occ_sb = keep.tile([P, S], F32)
-        nc.scalar.dma_start(out=occ_sb[:], in_=occ)
         corr_sb = keep.tile([P, V], F32)
-        nc.scalar.dma_start(out=corr_sb[:], in_=corr)
+        nc.sync.dma_start(out=corr_sb[:], in_=corr)
 
         ones = keep.tile([P, 1], F32)
         nc.gpsimd.memset(ones[:], 1.0)
@@ -56,13 +54,17 @@ def tile_picked_ylda_en_p_kernel(
         picked_scales = keep.tile([P, S], U8, align_bytes=64)
         nc.vector.tensor_copy(picked_scales[:], scale_table[:].indirect(offsets[:]))
         for j in range(4):
-            nc.sync.dma_start(
+            queue = nc.sync if j % 2 == 0 else nc.scalar
+            queue.dma_start(
                 out=x_scale_plane[j:P:32, :].bitcast(I32),
                 in_=picked_scales[P - 16 + j : P : 4, :].bitcast(I32),
             )
 
         w_bf = keep.tile([P, M, PACK], BF16, align_bytes=64)
-        nc.scalar.copy(out=w_bf[:], in_=w_raw[:].rearrange("p j m -> p m j"))
+        nc.vector.tensor_copy(out=w_bf[:], in_=w_raw[:].rearrange("p j m -> p m j"))
+        occ_sb = keep.tile([P, S], F32, tag="staging")
+        for half in (slice(0, S // 2), slice(S // 2, S)):
+            nc.sync.dma_start(out=occ_sb[:, half], in_=occ[:, half])
         w_codes = keep.tile([P, M], U32, align_bytes=64)
         w_scales = keep.tile([P, M], U8, align_bytes=64)
         nc.vector.quantize_mx(

from contextlib import ExitStack

import concourse.mybir as mybir

K, T, S, D, M, V = 512, 2048, 512, 8, 128, 64
FLOPS = 2 * K * M * S

F32 = mybir.dt.float32
BF16 = mybir.dt.bfloat16
I32 = mybir.dt.int32
U32 = mybir.dt.uint32
U16 = mybir.dt.uint16
U8 = mybir.dt.uint8
FP8X4 = mybir.dt.float8_e4m3fn_x4
ALU = mybir.AluOpType
ACT = mybir.ActivationFunctionType
AXIS = mybir.AxisListType

P = 128
PACK = 4
PIECE = 128
LIST_ROWS = 16


def tile_picked_ylda_en_p_kernel(
    tc, x_words, x_scales, w1, occ, corr, offs, out
):
    nc = tc.nc
    with ExitStack() as ctx:
        keep = ctx.enter_context(tc.tile_pool(name="keep", bufs=1))
        psum = ctx.enter_context(tc.psum_pool(name="psum", bufs=1))

        scale_table = keep.tile([P, T], U8, align_bytes=64)
        nc.scalar.dma_start(out=scale_table[P - 16 :, :].bitcast(I32), in_=x_scales[0].bitcast(I32))
        offsets = keep.tile([P, S // LIST_ROWS], U16)
        nc.sync.dma_start(offsets[:], offs)
        nc.vector.memset(scale_table[: P - 16, :].bitcast(I32), 0)
        x_scale_plane = keep.tile([P, S], U8, align_bytes=64)
        nc.vector.memset(x_scale_plane[:].bitcast(I32), 0)
        w_raw = keep.tile([P, PACK, M], F32, tag="staging")
        nc.sync.dma_start(out=w_raw[:], in_=w1.rearrange("(p j) m -> p j m", j=PACK))
        word_table = keep.tile([P, T], I32, align_bytes=64)
        nc.sync.dma_start(
            out=word_table[:], in_=x_words[0].rearrange("p n t -> p (n t)").bitcast(I32)
        )
        corr_sb = keep.tile([P, V], F32)
        nc.sync.dma_start(out=corr_sb[:], in_=corr)

        ones = keep.tile([P, 1], F32)
        nc.gpsimd.memset(ones[:], 1.0)
        tanh_bias = keep.tile([P, 1], F32)
        nc.scalar.activation(out=tanh_bias[:], in_=ones[:], func=ACT.Ln, scale=(0.8 / 0.62) ** 0.5)

        picked_scales = keep.tile([P, S], U8, align_bytes=64)
        nc.vector.tensor_copy(picked_scales[:], scale_table[:].indirect(offsets[:]))
        for j in range(4):
            queue = nc.sync if j % 2 == 0 else nc.scalar
            queue.dma_start(
                out=x_scale_plane[j:P:32, :].bitcast(I32),
                in_=picked_scales[P - 16 + j : P : 4, :].bitcast(I32),
            )

        w_bf = keep.tile([P, M, PACK], BF16, align_bytes=64)
        nc.vector.tensor_copy(out=w_bf[:], in_=w_raw[:].rearrange("p j m -> p m j"))
        occ_sb = keep.tile([P, S], F32, tag="staging")
        for half in (slice(0, S // 2), slice(S // 2, S)):
            nc.sync.dma_start(out=occ_sb[:, half], in_=occ[:, half])
        w_codes = keep.tile([P, M], U32, align_bytes=64)
        w_scales = keep.tile([P, M], U8, align_bytes=64)
        nc.vector.quantize_mx(
            out=w_codes[:].bitcast(FP8X4),
            scales=w_scales[:],
            in_=w_bf[:].rearrange("p m j -> p (m j)"),
        )


        pieces = range(S // PIECE)
        x_codes = [keep.tile([P, PIECE], U32, align_bytes=64, name=f"x_codes{i}") for i in pieces]
        for i in pieces:
            cols = slice(i * PIECE // LIST_ROWS, (i + 1) * PIECE // LIST_ROWS)
            nc.vector.tensor_copy(x_codes[i][:], word_table[:].bitcast(U32).indirect(offsets[:, cols]))

        sums = keep.tile([P, V], F32)
        weighted_tiles = []

        def add_up(i):
            nc.vector.tensor_reduce(
                out=sums[:, i * PIECE // D : (i + 1) * PIECE // D],
                in_=weighted_tiles[i][:].rearrange("p (v d) -> p v d", d=D),
                axis=AXIS.X,
                op=ALU.add,
            )

        for i in pieces:
            cols = slice(i * PIECE, (i + 1) * PIECE)
            y = psum.tile([M, PIECE], F32, name=f"y{i}")
            nc.tensor.matmul_mx(
                out=y[:],
                lhsT=w_codes[:].bitcast(FP8X4),
                lhsT_scale=w_scales[:],
                rhs=x_codes[i][:].bitcast(FP8X4),
                rhs_scale=x_scale_plane[:, cols],
                start=True,
                stop=True,
            )
            squares = keep.tile([M, PIECE], F32, name=f"squares{i}")
            nc.scalar.activation(out=squares[:], in_=y[:], func=ACT.Square)
            weighted = keep.tile([M, PIECE], F32, name=f"weighted{i}")
            nc.vector.tensor_tensor(weighted[:], squares[:], occ_sb[:, cols], ALU.mult)
            weighted_tiles.append(weighted)
            if i > 0:
                add_up(i - 1)
        add_up(pieces[-1])

        log_dens = keep.tile([M, V], F32)
        nc.scalar.activation(out=log_dens[:], in_=sums[:], func=ACT.Ln, bias=0.02)
        dens_corr = keep.tile([M, V], F32)
        nc.vector.scalar_tensor_tensor(dens_corr[:], sums[:], 0.02, corr_sb[:], ALU.add, ALU.mult)
        half_limit = keep.tile([M, V], F32)
        nc.vector.tensor_scalar(half_limit[:], dens_corr[:], -0.5 / 0.8, None, ALU.mult)

        tanh_term = keep.tile([M, V], F32)
        nc.scalar.activation(
            out=tanh_term[:], in_=log_dens[:], func=ACT.Tanh, scale=0.3333 / 2, bias=tanh_bias[:]
        )
        power = keep.tile([M, V], F32)
        nc.scalar.activation(out=power[:], in_=log_dens[:], func=ACT.Exp, scale=1.3333)
        correlation = keep.tile([M, V], F32)
        nc.vector.scalar_tensor_tensor(correlation[:], tanh_term[:], 1.0, half_limit[:], ALU.add, ALU.mult)
        result = keep.tile([M, V], F32)
        nc.vector.scalar_tensor_tensor(result[:], power[:], -0.738, correlation[:], ALU.mult, ALU.add)
        nc.sync.dma_start(out=out, in_=result[:])
